import numpy as np
import ml_dtypes


def mxq(x, axis, fmt="e4m3"):
    dtype, down = {"e4m3": (ml_dtypes.float8_e4m3fn, 7), "e5m2": (ml_dtypes.float8_e5m2, 14)}[fmt]
    v = np.moveaxis(np.asarray(x, np.float32).astype(ml_dtypes.bfloat16).astype(np.float64), axis, -1)
    blocks = v.reshape(v.shape[:-1] + (-1, 32))
    amax = np.abs(blocks).max(-1, keepdims=True)
    byte = np.maximum(np.where(amax > 0, np.frexp(amax)[1] - 1 + 127, 0) - down, 1)
    scale = np.exp2(byte - 127.0)
    codes = (blocks / scale).astype(np.float32).astype(dtype).astype(np.float64)
    return np.moveaxis((codes * scale).reshape(v.shape), -1, axis)


WIDE = False


def mx_kscale(k):
    if not WIDE:
        return np.ones(k)
    levels = np.array([10, -10, 5, -5, 0])
    if k % 512:
        return np.exp2(np.random.permutation(np.resize(levels, k // 32))).repeat(32)
    a = np.empty((k // 512, 16))
    for p in range(k // 512):
        a[p, :8] = np.random.permutation(np.resize(levels, 8))
        for g in range(8):
            far = levels[np.abs(levels - a[p, g]) >= 10]
            a[p, g + 8] = far[np.random.randint(len(far))]
    return np.exp2(a.ravel()).repeat(32)


def f64(x):
    return np.asarray(x).astype(np.float64)


def striped(idx):
    return np.tile(idx.reshape(-1, 16).T, (8, 1)).astype(np.uint16)


def unstriped(offs):
    return offs[:16].T.reshape(-1).astype(np.int64)


E2M1 = np.array([0.0, 0.5, 1.0, 1.5, 2.0, 3.0, 4.0, 6.0, -0.0, -0.5, -1.0, -1.5, -2.0, -3.0, -4.0, -6.0])


def pack_weight(w, fmt):
    k, n = w.shape
    w = f64(np.asarray(w, np.float32).astype(ml_dtypes.bfloat16)).reshape(k // 32, 32, n)
    amax = np.abs(w).max(1)
    if fmt == "e4m3":
        byte = np.frexp(amax)[1] - 1 + 127 - 7
    else:
        mant, ex = np.frexp(amax / 6.0)
        byte = np.where(mant > 0.5, ex, ex - 1) + 127
    byte = np.clip(np.where(amax > 0, byte, 1), 1, 254)
    scaled = (w * np.exp2(127.0 - byte)[:, None, :]).reshape(k, n).astype(np.float32)
    by_word = np.ascontiguousarray(scaled.reshape(k // 512, 128, 4, n).transpose(0, 1, 3, 2))
    if fmt == "e4m3":
        words = by_word.astype(ml_dtypes.float8_e4m3fn).view(np.uint8)
    else:
        c = by_word.astype(ml_dtypes.float4_e2m1fn).view(np.uint8) & 0xF
        words = (c[..., 0::2] | (c[..., 1::2] << 4)).reshape(k // 512, 128, 2 * n)
    return np.ascontiguousarray(words), np.ascontiguousarray(byte.astype(np.uint8).reshape(k // 512, 16, n))


def unpack_weight(words, scales, fmt):
    g, _, n = scales.shape
    words = np.ascontiguousarray(words).reshape(g, 128, n, -1)
    if fmt == "e4m3":
        vals = words.view(ml_dtypes.float8_e4m3fn).astype(np.float64)
    else:
        nib = np.empty((g, 128, n, 4), np.uint8)
        nib[..., 0::2] = words & 0xF
        nib[..., 1::2] = words >> 4
        vals = E2M1[nib]
    vals = vals * np.repeat(np.exp2(scales.astype(np.float64) - 127.0), 8, axis=1)[..., None]
    return vals.transpose(0, 1, 3, 2).reshape(g * 512, n)


K, T, E1, C1, E2, C2, H = 1536, 1024, 4, 256, 8, 128, 512
N = 512


def deal(E, C):
    slot_token = np.random.permutation(T)
    return slot_token, None, np.random.uniform(0.2, 1.0, T)


def by_expert(wq, xq, E, C):
    return np.concatenate([wq[e].T @ xq[:, e * C:(e + 1) * C] for e in range(E)], axis=1)


def setup_inputs():
    n = np.random.standard_normal
    s = mx_kscale(K)
    u = mx_kscale(H)
    slots1, pos1, g1 = deal(E1, C1)
    slots2, pos2, g2 = deal(E2, C2)
    x = pack_weight(n((K, T)) * s[:, None], "e4m3")
    w2 = [pack_weight(m, "e2m1") for m in n((E2, H, N)) / np.sqrt(H) / u[None, :, None]]
    return {
        "x_words": x[0],
        "x_scales": x[1],
        "w1": (n((E1, K, H)) / np.sqrt(K) / s[None, :, None] * u).astype(np.float32),
        "w2_words": np.stack([m[0] for m in w2]),
        "w2_scales": np.stack([m[1] for m in w2]),
        "gate1": (np.tile(g1, (128, 1))).astype(np.float32),
        "gate2": (np.tile(g2, (128, 1))).astype(np.float32),
        "offs": striped(slots1),
        "offs2": striped(slots2),
    }


def reference(x_words, x_scales, w1, w2_words, w2_scales, gate1, gate2, offs, offs2):
    w1q = mxq(f64(w1), 1, "e4m3")
    w2 = np.stack([unpack_weight(w2_words[e], w2_scales[e], "e2m1") for e in range(E2)])
    idx, idx2 = unstriped(offs), unstriped(offs2)
    xq = unpack_weight(x_words, x_scales, "e4m3")[:, idx]
    h = by_expert(w1q, xq, E1, C1)
    c = np.zeros((H, T))
    c[:, idx] = f64(gate1[:1]) * h
    y = by_expert(w2, mxq(c[:, idx2], 0, "e4m3"), E2, C2)
    out = np.zeros((N, T))
    out[:, idx2] = f64(gate2[:1]) * y
    return out

@@ -1,0 +1,238 @@
+from contextlib import ExitStack
+
+import concourse.mybir as mybir
+
+K, T, H, N = 1536, 1024, 512, 512
+E1, C1, E2, C2 = 4, 256, 8, 128
+FLOPS = 2 * T * (K * H + H * N)
+
+F32 = mybir.dt.float32
+BF16 = mybir.dt.bfloat16
+I32 = mybir.dt.int32
+U32 = mybir.dt.uint32
+U16 = mybir.dt.uint16
+U8 = mybir.dt.uint8
+FP8X4 = mybir.dt.float8_e4m3fn_x4
+FP4X4 = mybir.dt.float4_e2m1fn_x4
+COPY = mybir.ActivationFunctionType.Copy
+MULT = mybir.AluOpType.mult
+
+P = 128
+PASSES = K // 512
+HALF = H // 2
+SLAB = 4096
+PARTS = ((0, C1), (C1, T))
+CHUNKS = ((0, 1), (1, 2), (2, 4), (4, 6), (6, 8))
+
+
+def cols16(lo, hi):
+    return slice(lo // 16, hi // 16)
+
+
+def tile_moe_ser_none_kernel(
+    tc, x_words, x_scales, w1, w2_words, w2_scales, gate1, gate2, offs, offs2, out
+):
+    nc = tc.nc
+    with ExitStack() as ctx:
+        keep = ctx.enter_context(tc.tile_pool(name="keep", bufs=1))
+        loads = ctx.enter_context(tc.tile_pool(name="loads", bufs=10))
+        ring = ctx.enter_context(tc.tile_pool(name="ring", bufs=3))
+        ring4 = ctx.enter_context(tc.tile_pool(name="ring4", bufs=4))
+        shared = ctx.enter_context(tc.tile_pool(name="shared", bufs=1))
+        psum = ctx.enter_context(tc.psum_pool(name="psum", bufs=2))
+
+        list1 = keep.tile([P, T // 16], U16, name="list1")
+        list2 = keep.tile([P, T // 16], U16, name="list2")
+        xw = [shared.tile([P, T], I32, name="xw0", align_bytes=64, offset=0)]
+        xw += [keep.tile([P, T], I32, name="xw%d" % a, align_bytes=64) for a in range(1, PASSES)]
+        xs = keep.tile([P, T], U8, name="xs", align_bytes=64)
+        w2w = keep.tile([P, E2 * 2 * N], U8, name="w2w", align_bytes=64)
+        w2s = keep.tile([P, E2 * N], U8, name="w2s", align_bytes=64)
+        g1 = [keep.tile([P, C1], F32, name="g1_%d" % e) for e in range(E1)]
+        g2 = keep.tile([P, T], F32, name="g2")
+
+        nc.gpsimd.memset(xs[:].bitcast(I32), 0)
+        nc.vector.memset(w2s[:].bitcast(I32), 0)
+
+        raw = {}
+
+        def load_w1(e, a, hf=None):
+            rows = w1[e, 512 * a : 512 * (a + 1), :].rearrange("(p j) n -> p j n", j=4)
+            if hf != 1:
+                raw[(e, a)] = loads.tile([P, 4, H], F32, name="raw")
+            cols = slice(0, H) if hf is None else slice(hf * HALF, (hf + 1) * HALF)
+            nc.sync.dma_start(out=raw[(e, a)][:, :, cols], in_=rows[:, :, cols])
+
+        def load_xw(a):
+            nc.sync.dma_start(out=xw[a][:], in_=x_words[a].rearrange("p t d -> p (t d)").bitcast(I32))
+
+        nc.sync.dma_start(list1[:], offs)
+        for q in range(4):
+            nc.gpsimd.dma_start(
+                out=xs[32 * q : 32 * q + 4 * PASSES, :].bitcast(I32),
+                in_=x_scales[:, 4 * q : 4 * q + 4, :].bitcast(I32),
+            )
+        load_xw(0)
+        load_w1(0, 0)
+        load_xw(1)
+        load_w1(0, 1)
+        load_w1(0, 2, 0)
+        load_w1(0, 2, 1)
+        load_xw(2)
+        nc.sync.dma_start(out=g1[0][:], in_=gate1[:, 0:C1])
+        for e in range(1, E1):
+            for a in range(PASSES):
+                load_w1(e, a)
+            nc.sync.dma_start(out=g1[e][:], in_=gate1[:, e * C1 : (e + 1) * C1])
+        nc.sync.dma_start(list2[:], offs2)
+        for q in range(4):
+            nc.sync.dma_start(
+                out=w2s[32 * q : 32 * q + 4, :].bitcast(I32).rearrange("r (f n) -> r f n", f=E2),
+                in_=w2_scales[:, 0, 4 * q : 4 * q + 4, :].bitcast(I32).rearrange("f r n -> r f n"),
+            )
+        nc.sync.dma_start(
+            out=w2w[:].bitcast(I32).rearrange("p (f n) -> p f n", f=E2),
+            in_=w2_words[:, 0, :, :].bitcast(I32).rearrange("f p n -> p f n"),
+        )
+        nc.sync.dma_start(out=g2[:], in_=gate2)
+
+        gw = {}
+        gs = {}
+
+        def gather_words(a, half):
+            lo, hi = PARTS[half]
+            if a == PASSES - 1:
+                t = shared.tile([P, hi - lo], U32, name="gw%d_%d" % (a, half), align_bytes=64, offset=SLAB * (1 + half))
+            else:
+                t = keep.tile([P, hi - lo], U32, name="gw%d_%d" % (a, half), align_bytes=64)
+            nc.vector.tensor_copy(t[:], xw[a][:].bitcast(U32).indirect(list1[:, cols16(lo, hi)]))
+            gw[(a, half)] = t
+
+        def gather_scales(half):
+            lo, hi = PARTS[half]
+            t = shared.tile([P, hi - lo], U8, name="gs%d" % half, align_bytes=64, offset=lo)
+            nc.vector.tensor_copy(t[:], xs[:].indirect(list1[:, cols16(lo, hi)]))
+            gs[half] = t
+
+        cw = [keep.tile([P, T], F32, name="cw%d" % t) for t in range(4)]
+        cb = [keep.tile([P, T], BF16, name="cb%d" % t) for t in range(4)]
+        accs = {}
+
+        def regroup(copy, stage, e, a, lo, hi):
+            copy(
+                stage[:, :, lo // 4 : hi // 4, :].rearrange("p t m j -> p m j t"),
+                raw[(e, a)][:, :, lo:hi].rearrange("p j (m t) -> p m j t", t=4),
+            )
+
+        def pass1(e, a):
+            if e == 0 and a > 0:
+                stage = shared.tile([P, 4, P, 4], BF16, name="stage0_%d" % a, align_bytes=64, offset=SLAB * a)
+            else:
+                stage = ring4.tile([P, 4, P, 4], BF16, name="stage", align_bytes=64)
+            regroup(nc.scalar.copy, stage, e, a, 0, HALF)
+            regroup(nc.vector.tensor_copy if (e, a) == (0, 2) else nc.scalar.copy, stage, e, a, HALF, H)
+            codes = ring4.tile([P, H], U32, name="w1c", align_bytes=64)
+            scales = ring4.tile([P, H], U8, name="w1s", align_bytes=64)
+            nc.vector.quantize_mx(
+                out=codes[:].bitcast(FP8X4), scales=scales[:], in_=stage[:].rearrange("p t m j -> p (t m j)")
+            )
+            half = min(e, 1)
+            at = e * C1 - PARTS[half][0]
+            for t in range(4):
+                if a == 0:
+                    accs[(e, t)] = psum.tile([P, C1], F32, name="bank%d" % t)
+                nc.tensor.matmul_mx(
+                    out=accs[(e, t)][:],
+                    lhsT=codes[:, t * P : (t + 1) * P].bitcast(FP8X4),
+                    lhsT_scale=scales[:, t * P : (t + 1) * P],
+                    rhs=gw[(a, half)][:, at : at + C1].bitcast(FP8X4),
+                    rhs_scale=gs[half][4 * a : P, at : at + C1],
+                    start=(a == 0),
+                    stop=(a == PASSES - 1),
+                )
+
+        def back1(e, t):
+            if t == 3 and e + 1 < E1:
+                h = raw[(e + 1, PASSES - 1)][:, 3, H - C1 : H]
+            else:
+                h = ring4.tile([P, C1], F32, name="h")[:]
+            nc.scalar.copy(h, accs[(e, t)][:])
+            nc.vector.tensor_tensor(cw[t][:].indirect(list1[:, cols16(e * C1, (e + 1) * C1)]), h, g1[e][:], MULT)
+
+        cq_in = {}
+
+        def gather2(c, t):
+            lo, hi = CHUNKS[c][0] * C2, CHUNKS[c][1] * C2
+            if t == 0:
+                cq_in[c] = ring.tile([P, hi - lo, 4], BF16, name="cq_in", align_bytes=64)
+            nc.scalar.activation(cq_in[c][:, :, t], cb[t][:].indirect(list2[:, cols16(lo, hi)]), COPY)
+
+        acc2 = {}
+
+        def layer2(c):
+            width = (CHUNKS[c][1] - CHUNKS[c][0]) * C2
+            cq = ring.tile([P, width], U32, name="cq", align_bytes=64)
+            cs = ring.tile([P, width], U8, name="cs", align_bytes=64)
+            nc.vector.quantize_mx(out=cq[:].bitcast(FP8X4), scales=cs[:], in_=cq_in[c][:].rearrange("p m t -> p (m t)"))
+            for i, f in enumerate(range(*CHUNKS[c])):
+                acc2[f] = psum.tile([P, 4, C2], F32, name="bank%d" % (f % 4))
+                for nt in range(4):
+                    nc.tensor.matmul_mx(
+                        out=acc2[f][:, nt, :],
+                        lhsT=w2w[:, f * 2 * N + nt * 2 * P : f * 2 * N + (nt + 1) * 2 * P].bitcast(FP4X4),
+                        lhsT_scale=w2s[:, f * N + nt * P : f * N + (nt + 1) * P],
+                        rhs=cq[:, i * C2 : (i + 1) * C2].bitcast(FP8X4),
+                        rhs_scale=cs[:, i * C2 : (i + 1) * C2],
+                        start=True,
+                        stop=True,
+                    )
+
+        ow = [keep.tile([P, T], F32, name="ow%d" % nt) for nt in range(4)]
+
+        def back2(c):
+            lo, hi = CHUNKS[c][0] * C2, CHUNKS[c][1] * C2
+            y = ring.tile([P, 4, hi - lo], F32, name="y")
+            for i, f in enumerate(range(*CHUNKS[c])):
+                nc.scalar.copy(y[:, :, i * C2 : (i + 1) * C2], acc2[f][:])
+            for nt in range(4):
+                nc.vector.tensor_tensor(ow[nt][:].indirect(list2[:, cols16(lo, hi)]), y[:, nt, :], g2[:, lo:hi], MULT)
+                if c == len(CHUNKS) - 1:
+                    nc.sync.dma_start(out=out[nt * P : (nt + 1) * P, :], in_=ow[nt][:])
+
+        gather_words(0, 0)
+        gather_words(0, 1)
+        gather_scales(0)
+        gather_scales(1)
+        gather_words(1, 0)
+        gather_words(1, 1)
+        pass1(0, 0)
+        pass1(0, 1)
+        gather_words(2, 0)
+        pass1(0, 2)
+        gather_words(2, 1)
+        for e in range(E1 - 1):
+            back1(e, 0)
+            back1(e, 1)
+            if e == 0:
+                pass1(1, 0)
+            pass1(e + 1, 1)
+            back1(e, 2)
+            pass1(e + 1, 2)
+            back1(e, 3)
+            if e + 2 < E1:
+                pass1(e + 2, 0)
+        for t in range(4):
+            back1(E1 - 1, t)
+        for t in range(4):
+            if t < 3:
+                nc.scalar.copy(cb[t][:], cw[t][:])
+            else:
+                nc.vector.tensor_copy(cb[t][:], cw[t][:])
+            gather2(0, t)
+        layer2(0)
+        for c in range(len(CHUNKS)):
+            if c + 1 < len(CHUNKS):
+                for t in range(4):
+                    gather2(c + 1, t)
+                layer2(c + 1)
+            back2(c)

@@ -51,7 +51,7 @@ def tile_moe_ser_none_kernel(
         g1 = [keep.tile([P, C1], F32, name="g1_%d" % e) for e in range(E1)]
         g2 = keep.tile([P, T], F32, name="g2")
 
-        nc.gpsimd.memset(xs[:].bitcast(I32), 0)
+        nc.vector.memset(xs[:].bitcast(I32), 0)
         nc.vector.memset(w2s[:].bitcast(I32), 0)
 
         raw = {}
@@ -67,23 +67,25 @@ def tile_moe_ser_none_kernel(
             nc.sync.dma_start(out=xw[a][:], in_=x_words[a].rearrange("p t d -> p (t d)").bitcast(I32))
 
         nc.sync.dma_start(list1[:], offs)
-        for q in range(4):
-            nc.gpsimd.dma_start(
-                out=xs[32 * q : 32 * q + 4 * PASSES, :].bitcast(I32),
-                in_=x_scales[:, 4 * q : 4 * q + 4, :].bitcast(I32),
-            )
         load_xw(0)
         load_w1(0, 0)
+        for q in range(4):
+            for lo, hi in ((0, 2), (2, 3)):
+                nc.sync.dma_start(
+                    out=xs[32 * q + 4 * lo : 32 * q + 4 * hi, :].bitcast(I32),
+                    in_=x_scales[lo:hi, 4 * q : 4 * q + 4, :].bitcast(I32),
+                )
         load_xw(1)
         load_w1(0, 1)
         load_w1(0, 2, 0)
         load_w1(0, 2, 1)
         load_xw(2)
-        nc.sync.dma_start(out=g1[0][:], in_=gate1[:, 0:C1])
-        for e in range(1, E1):
+        for e in range(1, E1 + 1):
             for a in range(PASSES):
-                load_w1(e, a)
-            nc.sync.dma_start(out=g1[e][:], in_=gate1[:, e * C1 : (e + 1) * C1])
+                if e < E1:
+                    load_w1(e, a)
+                if a == 0:
+                    nc.sync.dma_start(out=g1[e - 1][:], in_=gate1[:, (e - 1) * C1 : e * C1])
         nc.sync.dma_start(list2[:], offs2)
         for q in range(4):
             nc.sync.dma_start(
@@ -129,8 +131,15 @@ def tile_moe_ser_none_kernel(
                 stage = shared.tile([P, 4, P, 4], BF16, name="stage0_%d" % a, align_bytes=64, offset=SLAB * a)
             else:
                 stage = ring4.tile([P, 4, P, 4], BF16, name="stage", align_bytes=64)
-            regroup(nc.scalar.copy, stage, e, a, 0, HALF)
-            regroup(nc.vector.tensor_copy if (e, a) == (0, 2) else nc.scalar.copy, stage, e, a, HALF, H)
+            if (e, a) == (0, 2):
+                regroup(nc.scalar.copy, stage, e, a, 0, HALF)
+                regroup(nc.vector.tensor_copy, stage, e, a, HALF, H)
+            else:
+                for t in (0, 2):
+                    nc.scalar.copy(
+                        stage[:, t : t + 2, :, :].rearrange("p t m j -> p m j t"),
+                        raw[(e, a)][:].rearrange("p j (m t) -> p m j t", t=4)[:, :, :, t : t + 2],
+                    )
             codes = ring4.tile([P, H], U32, name="w1c", align_bytes=64)
             scales = ring4.tile([P, H], U8, name="w1s", align_bytes=64)
             nc.vector.quantize_mx(
@@ -165,7 +174,10 @@ def tile_moe_ser_none_kernel(
             lo, hi = CHUNKS[c][0] * C2, CHUNKS[c][1] * C2
             if t == 0:
                 cq_in[c] = ring.tile([P, hi - lo, 4], BF16, name="cq_in", align_bytes=64)
-            nc.scalar.activation(cq_in[c][:, :, t], cb[t][:].indirect(list2[:, cols16(lo, hi)]), COPY)
+            if c == 0 and t >= 2:
+                nc.vector.tensor_copy(cq_in[c][:, :, t], cw[t][:].indirect(list2[:, cols16(lo, hi)]))
+            else:
+                nc.scalar.activation(cq_in[c][:, :, t], cb[t][:].indirect(list2[:, cols16(lo, hi)]), COPY)
 
         acc2 = {}
 
@@ -189,13 +201,13 @@ def tile_moe_ser_none_kernel(
 
         ow = [keep.tile([P, T], F32, name="ow%d" % nt) for nt in range(4)]
 
-        def back2(c):
+        def back2(c, pair):
             lo, hi = CHUNKS[c][0] * C2, CHUNKS[c][1] * C2
-            y = ring.tile([P, 4, hi - lo], F32, name="y")
+            y = ring4.tile([P, 2, hi - lo], F32, name="y")
             for i, f in enumerate(range(*CHUNKS[c])):
-                nc.scalar.copy(y[:, :, i * C2 : (i + 1) * C2], acc2[f][:])
-            for nt in range(4):
-                nc.vector.tensor_tensor(ow[nt][:].indirect(list2[:, cols16(lo, hi)]), y[:, nt, :], g2[:, lo:hi], MULT)
+                nc.scalar.copy(y[:, :, i * C2 : (i + 1) * C2], acc2[f][:, 2 * pair : 2 * pair + 2, :])
+            for nt in range(2 * pair, 2 * pair + 2):
+                nc.vector.tensor_tensor(ow[nt][:].indirect(list2[:, cols16(lo, hi)]), y[:, nt % 2, :], g2[:, lo:hi], MULT)
                 if c == len(CHUNKS) - 1:
                     nc.sync.dma_start(out=out[nt * P : (nt + 1) * P, :], in_=ow[nt][:])
 
@@ -224,15 +236,13 @@ def tile_moe_ser_none_kernel(
         for t in range(4):
             back1(E1 - 1, t)
         for t in range(4):
-            if t < 3:
-                nc.scalar.copy(cb[t][:], cw[t][:])
-            else:
-                nc.vector.tensor_copy(cb[t][:], cw[t][:])
+            nc.scalar.copy(cb[t][:], cw[t][:])
             gather2(0, t)
         layer2(0)
         for c in range(len(CHUNKS)):
+            back2(c, 0)
             if c + 1 < len(CHUNKS):
                 for t in range(4):
                     gather2(c + 1, t)
                 layer2(c + 1)
-            back2(c)
+            back2(c, 1)

@@ -43,8 +43,11 @@ def tile_moe_ser_none_kernel(
 
         list1 = keep.tile([P, T // 16], U16, name="list1")
         list2 = keep.tile([P, T // 16], U16, name="list2")
-        xw = [shared.tile([P, T], I32, name="xw0", align_bytes=64, offset=0)]
-        xw += [keep.tile([P, T], I32, name="xw%d" % a, align_bytes=64) for a in range(1, PASSES)]
+        xw = [
+            keep.tile([P, T], I32, name="xw0", align_bytes=64),
+            shared.tile([P, T], I32, name="xw1", align_bytes=64, offset=0),
+            keep.tile([P, T], I32, name="xw2", align_bytes=64),
+        ]
         xs = keep.tile([P, T], U8, name="xs", align_bytes=64)
         w2w = keep.tile([P, E2 * 2 * N], U8, name="w2w", align_bytes=64)
         w2s = keep.tile([P, E2 * N], U8, name="w2s", align_bytes=64)
@@ -66,8 +69,9 @@ def tile_moe_ser_none_kernel(
         def load_xw(a):
             nc.sync.dma_start(out=xw[a][:], in_=x_words[a].rearrange("p t d -> p (t d)").bitcast(I32))
 
-        nc.sync.dma_start(list1[:], offs)
         load_xw(0)
+        nc.sync.dma_start(list1[:], offs)
+        load_xw(1)
         load_w1(0, 0)
         for q in range(4):
             for lo, hi in ((0, 2), (2, 3)):
@@ -75,7 +79,6 @@ def tile_moe_ser_none_kernel(
                     out=xs[32 * q + 4 * lo : 32 * q + 4 * hi, :].bitcast(I32),
                     in_=x_scales[lo:hi, 4 * q : 4 * q + 4, :].bitcast(I32),
                 )
-        load_xw(1)
         load_w1(0, 1)
         load_w1(0, 2, 0)
         load_w1(0, 2, 1)
@@ -213,10 +216,10 @@ def tile_moe_ser_none_kernel(
 
         gather_words(0, 0)
         gather_words(0, 1)
-        gather_scales(0)
-        gather_scales(1)
         gather_words(1, 0)
         gather_words(1, 1)
+        gather_scales(0)
+        gather_scales(1)
         pass1(0, 0)
         pass1(0, 1)
         gather_words(2, 0)

@@ -18,14 +18,23 @@ COPY = mybir.ActivationFunctionType.Copy
 MULT = mybir.AluOpType.mult
 
 P = 128
-PASSES = K // 512
+PACK = 4
+K_PASS = P * PACK
+PASSES = K // K_PASS
+LAST_PASS = PASSES - 1
 HALF = H // 2
+QUADRANTS = 4
+ALIGN = 64
 SLAB = 4096
+
 PARTS = ((0, C1), (C1, T))
 CHUNKS = ((0, 1), (1, 2), (2, 4), (4, 6), (6, 8))
+EARLY_CHUNKS = 2
+HALVED = ((0, LAST_PASS), (1, 0))
+ON_VECTOR = ((0, LAST_PASS, 1), (2, 1, 1))
 
 
-def cols16(lo, hi):
+def entries(lo, hi):
     return slice(lo // 16, hi // 16)
 
 
@@ -36,7 +45,7 @@ def tile_moe_ser_none_kernel(
     with ExitStack() as ctx:
         keep = ctx.enter_context(tc.tile_pool(name="keep", bufs=1))
         loads = ctx.enter_context(tc.tile_pool(name="loads", bufs=10))
-        ring = ctx.enter_context(tc.tile_pool(name="ring", bufs=3))
+        ring3 = ctx.enter_context(tc.tile_pool(name="ring3", bufs=3))
         ring4 = ctx.enter_context(tc.tile_pool(name="ring4", bufs=4))
         shared = ctx.enter_context(tc.tile_pool(name="shared", bufs=1))
         psum = ctx.enter_context(tc.psum_pool(name="psum", bufs=2))
@@ -44,13 +53,13 @@ def tile_moe_ser_none_kernel(
         list1 = keep.tile([P, T // 16], U16, name="list1")
         list2 = keep.tile([P, T // 16], U16, name="list2")
         xw = [
-            keep.tile([P, T], I32, name="xw0", align_bytes=64),
-            shared.tile([P, T], I32, name="xw1", align_bytes=64, offset=0),
-            keep.tile([P, T], I32, name="xw2", align_bytes=64),
+            keep.tile([P, T], I32, name="xw0", align_bytes=ALIGN),
+            shared.tile([P, T], I32, name="xw1", align_bytes=ALIGN, offset=0),
+            keep.tile([P, T], I32, name="xw2", align_bytes=ALIGN),
         ]
-        xs = keep.tile([P, T], U8, name="xs", align_bytes=64)
-        w2w = keep.tile([P, E2 * 2 * N], U8, name="w2w", align_bytes=64)
-        w2s = keep.tile([P, E2 * N], U8, name="w2s", align_bytes=64)
+        xs = keep.tile([P, T], U8, name="xs", align_bytes=ALIGN)
+        w2w = keep.tile([P, E2 * 2 * N], U8, name="w2w", align_bytes=ALIGN)
+        w2s = keep.tile([P, E2 * N], U8, name="w2s", align_bytes=ALIGN)
         g1 = [keep.tile([P, C1], F32, name="g1_%d" % e) for e in range(E1)]
         g2 = keep.tile([P, T], F32, name="g2")
 
@@ -59,38 +68,46 @@ def tile_moe_ser_none_kernel(
 
         raw = {}
 
-        def load_w1(e, a, hf=None):
-            rows = w1[e, 512 * a : 512 * (a + 1), :].rearrange("(p j) n -> p j n", j=4)
-            if hf != 1:
-                raw[(e, a)] = loads.tile([P, 4, H], F32, name="raw")
-            cols = slice(0, H) if hf is None else slice(hf * HALF, (hf + 1) * HALF)
+        def load_w1(e, a, half=None):
+            rows = w1[e, K_PASS * a : K_PASS * (a + 1), :].rearrange("(p j) i -> p j i", j=PACK)
+            if half != 1:
+                raw[(e, a)] = loads.tile([P, PACK, H], F32, name="raw")
+            cols = slice(0, H) if half is None else slice(half * HALF, (half + 1) * HALF)
             nc.sync.dma_start(out=raw[(e, a)][:, :, cols], in_=rows[:, :, cols])
 
         def load_xw(a):
             nc.sync.dma_start(out=xw[a][:], in_=x_words[a].rearrange("p t d -> p (t d)").bitcast(I32))
 
-        load_xw(0)
-        nc.sync.dma_start(list1[:], offs)
-        load_xw(1)
-        load_w1(0, 0)
-        for q in range(4):
-            for lo, hi in ((0, 2), (2, 3)):
+        def load_xs(q):
+            for lo, hi in ((0, 2), (2, PASSES)):
                 nc.sync.dma_start(
                     out=xs[32 * q + 4 * lo : 32 * q + 4 * hi, :].bitcast(I32),
                     in_=x_scales[lo:hi, 4 * q : 4 * q + 4, :].bitcast(I32),
                 )
+
+        load_xw(0)
+        nc.sync.dma_start(list1[:], offs)
+        load_xs(0)
+        load_xw(1)
+        load_xs(1)
+        load_w1(0, 0)
+        load_xs(2)
+        load_xs(3)
         load_w1(0, 1)
-        load_w1(0, 2, 0)
-        load_w1(0, 2, 1)
-        load_xw(2)
-        for e in range(1, E1 + 1):
-            for a in range(PASSES):
-                if e < E1:
-                    load_w1(e, a)
-                if a == 0:
-                    nc.sync.dma_start(out=g1[e - 1][:], in_=gate1[:, (e - 1) * C1 : e * C1])
+        load_w1(0, LAST_PASS, 0)
+        load_w1(0, LAST_PASS, 1)
+        load_w1(1, 0, 0)
+        load_xw(LAST_PASS)
+        load_w1(1, 0, 1)
+        for e in range(E1):
+            nc.sync.dma_start(out=g1[e][:], in_=gate1[:, e * C1 : (e + 1) * C1])
+            if e + 1 < E1:
+                for a in range(1, PASSES):
+                    load_w1(e + 1, a)
+            if e + 2 < E1:
+                load_w1(e + 2, 0)
         nc.sync.dma_start(list2[:], offs2)
-        for q in range(4):
+        for q in range(QUADRANTS):
             nc.sync.dma_start(
                 out=w2s[32 * q : 32 * q + 4, :].bitcast(I32).rearrange("r (f n) -> r f n", f=E2),
                 in_=w2_scales[:, 0, 4 * q : 4 * q + 4, :].bitcast(I32).rearrange("f r n -> r f n"),
@@ -104,148 +121,145 @@ def tile_moe_ser_none_kernel(
         gw = {}
         gs = {}
 
-        def gather_words(a, half):
-            lo, hi = PARTS[half]
-            if a == PASSES - 1:
-                t = shared.tile([P, hi - lo], U32, name="gw%d_%d" % (a, half), align_bytes=64, offset=SLAB * (1 + half))
+        def gather_words(a, part):
+            lo, hi = PARTS[part]
+            name = "gw%d_%d" % (a, part)
+            if a == LAST_PASS:
+                gw[(a, part)] = shared.tile([P, hi - lo], U32, name=name, align_bytes=ALIGN, offset=SLAB * (1 + part))
             else:
-                t = keep.tile([P, hi - lo], U32, name="gw%d_%d" % (a, half), align_bytes=64)
-            nc.vector.tensor_copy(t[:], xw[a][:].bitcast(U32).indirect(list1[:, cols16(lo, hi)]))
-            gw[(a, half)] = t
+                gw[(a, part)] = keep.tile([P, hi - lo], U32, name=name, align_bytes=ALIGN)
+            nc.vector.tensor_copy(gw[(a, part)][:], xw[a][:].bitcast(U32).indirect(list1[:, entries(lo, hi)]))
 
-        def gather_scales(half):
-            lo, hi = PARTS[half]
-            t = shared.tile([P, hi - lo], U8, name="gs%d" % half, align_bytes=64, offset=lo)
-            nc.vector.tensor_copy(t[:], xs[:].indirect(list1[:, cols16(lo, hi)]))
-            gs[half] = t
+        def gather_scales(part):
+            lo, hi = PARTS[part]
+            gs[part] = shared.tile([P, hi - lo], U8, name="gs%d" % part, align_bytes=ALIGN, offset=lo)
+            nc.vector.tensor_copy(gs[part][:], xs[:].indirect(list1[:, entries(lo, hi)]))
 
-        cw = [keep.tile([P, T], F32, name="cw%d" % t) for t in range(4)]
-        cb = [keep.tile([P, T], BF16, name="cb%d" % t) for t in range(4)]
-        accs = {}
+        c32 = [keep.tile([P, T], F32, name="c32_%d" % t) for t in range(PACK)]
+        c16 = [keep.tile([P, T], BF16, name="c16_%d" % t) for t in range(PACK)]
+        acc1 = {}
 
-        def regroup(copy, stage, e, a, lo, hi):
-            copy(
-                stage[:, :, lo // 4 : hi // 4, :].rearrange("p t m j -> p m j t"),
-                raw[(e, a)][:, :, lo:hi].rearrange("p j (m t) -> p m j t", t=4),
-            )
-
-        def pass1(e, a):
+        def layer1_pass(e, a):
             if e == 0 and a > 0:
-                stage = shared.tile([P, 4, P, 4], BF16, name="stage0_%d" % a, align_bytes=64, offset=SLAB * a)
+                stage = shared.tile([P, PACK, P, PACK], BF16, name="stage0_%d" % a, align_bytes=ALIGN, offset=SLAB * a)
             else:
-                stage = ring4.tile([P, 4, P, 4], BF16, name="stage", align_bytes=64)
-            if (e, a) == (0, 2):
-                regroup(nc.scalar.copy, stage, e, a, 0, HALF)
-                regroup(nc.vector.tensor_copy, stage, e, a, HALF, H)
-            else:
-                for t in (0, 2):
-                    nc.scalar.copy(
-                        stage[:, t : t + 2, :, :].rearrange("p t m j -> p m j t"),
-                        raw[(e, a)][:].rearrange("p j (m t) -> p m j t", t=4)[:, :, :, t : t + 2],
-                    )
-            codes = ring4.tile([P, H], U32, name="w1c", align_bytes=64)
-            scales = ring4.tile([P, H], U8, name="w1s", align_bytes=64)
+                stage = ring4.tile([P, PACK, P, PACK], BF16, name="stage", align_bytes=ALIGN)
+            dst = stage[:].rearrange("p t m j -> p m j t")
+            src = raw[(e, a)][:].rearrange("p j (m t) -> p m j t", t=PACK)
+            for half in range(2):
+                copy = nc.vector.tensor_copy if (e, a, half) in ON_VECTOR else nc.scalar.copy
+                if (e, a) in HALVED:
+                    ms = slice(half * P // 2, (half + 1) * P // 2)
+                    copy(dst[:, ms, :, :], src[:, ms, :, :])
+                else:
+                    ts = slice(2 * half, 2 * half + 2)
+                    copy(dst[:, :, :, ts], src[:, :, :, ts])
+            codes = ring4.tile([P, H], U32, name="w1_codes", align_bytes=ALIGN)
+            scales = ring4.tile([P, H], U8, name="w1_scales", align_bytes=ALIGN)
             nc.vector.quantize_mx(
                 out=codes[:].bitcast(FP8X4), scales=scales[:], in_=stage[:].rearrange("p t m j -> p (t m j)")
             )
-            half = min(e, 1)
-            at = e * C1 - PARTS[half][0]
-            for t in range(4):
+            part = min(e, 1)
+            at = e * C1 - PARTS[part][0]
+            for t in range(PACK):
                 if a == 0:
-                    accs[(e, t)] = psum.tile([P, C1], F32, name="bank%d" % t)
+                    acc1[(e, t)] = psum.tile([P, C1], F32, name="bank%d" % t)
                 nc.tensor.matmul_mx(
-                    out=accs[(e, t)][:],
+                    out=acc1[(e, t)][:],
                     lhsT=codes[:, t * P : (t + 1) * P].bitcast(FP8X4),
                     lhsT_scale=scales[:, t * P : (t + 1) * P],
-                    rhs=gw[(a, half)][:, at : at + C1].bitcast(FP8X4),
-                    rhs_scale=gs[half][4 * a : P, at : at + C1],
+                    rhs=gw[(a, part)][:, at : at + C1].bitcast(FP8X4),
+                    rhs_scale=gs[part][4 * a : P, at : at + C1],
                     start=(a == 0),
-                    stop=(a == PASSES - 1),
+                    stop=(a == LAST_PASS),
                 )
 
-        def back1(e, t):
-            if t == 3 and e + 1 < E1:
-                h = raw[(e + 1, PASSES - 1)][:, 3, H - C1 : H]
+        def scatter1(e, t):
+            if t == PACK - 1 and e + 1 < E1:
+                h = raw[(e + 1, LAST_PASS)][:, PACK - 1, H - C1 : H]
             else:
                 h = ring4.tile([P, C1], F32, name="h")[:]
-            nc.scalar.copy(h, accs[(e, t)][:])
-            nc.vector.tensor_tensor(cw[t][:].indirect(list1[:, cols16(e * C1, (e + 1) * C1)]), h, g1[e][:], MULT)
+            nc.scalar.copy(h, acc1[(e, t)][:])
+            nc.vector.tensor_tensor(c32[t][:].indirect(list1[:, entries(e * C1, (e + 1) * C1)]), h, g1[e][:], MULT)
 
-        cq_in = {}
+        slots16 = {}
 
-        def gather2(c, t):
-            lo, hi = CHUNKS[c][0] * C2, CHUNKS[c][1] * C2
+        def gather2(ch, t):
+            lo, hi = CHUNKS[ch][0] * C2, CHUNKS[ch][1] * C2
             if t == 0:
-                cq_in[c] = ring.tile([P, hi - lo, 4], BF16, name="cq_in", align_bytes=64)
-            if c == 0 and t >= 2:
-                nc.vector.tensor_copy(cq_in[c][:, :, t], cw[t][:].indirect(list2[:, cols16(lo, hi)]))
+                slots16[ch] = ring3.tile([P, hi - lo, PACK], BF16, name="slots16", align_bytes=ALIGN)
+            if ch < EARLY_CHUNKS and t >= 2:
+                nc.vector.tensor_copy(slots16[ch][:, :, t], c32[t][:].indirect(list2[:, entries(lo, hi)]))
             else:
-                nc.scalar.activation(cq_in[c][:, :, t], cb[t][:].indirect(list2[:, cols16(lo, hi)]), COPY)
+                nc.scalar.activation(slots16[ch][:, :, t], c16[t][:].indirect(list2[:, entries(lo, hi)]), COPY)
 
         acc2 = {}
 
-        def layer2(c):
-            width = (CHUNKS[c][1] - CHUNKS[c][0]) * C2
-            cq = ring.tile([P, width], U32, name="cq", align_bytes=64)
-            cs = ring.tile([P, width], U8, name="cs", align_bytes=64)
-            nc.vector.quantize_mx(out=cq[:].bitcast(FP8X4), scales=cs[:], in_=cq_in[c][:].rearrange("p m t -> p (m t)"))
-            for i, f in enumerate(range(*CHUNKS[c])):
-                acc2[f] = psum.tile([P, 4, C2], F32, name="bank%d" % (f % 4))
-                for nt in range(4):
+        def layer2(ch):
+            width = (CHUNKS[ch][1] - CHUNKS[ch][0]) * C2
+            codes = ring3.tile([P, width], U32, name="c_codes", align_bytes=ALIGN)
+            scales = ring3.tile([P, width], U8, name="c_scales", align_bytes=ALIGN)
+            nc.vector.quantize_mx(
+                out=codes[:].bitcast(FP8X4), scales=scales[:], in_=slots16[ch][:].rearrange("p m t -> p (m t)")
+            )
+            for nth, f in enumerate(range(*CHUNKS[ch])):
+                acc2[f] = psum.tile([P, PACK, C2], F32, name="bank%d" % (f % PACK))
+                for r in range(PACK):
+                    col = f * N + r * P
                     nc.tensor.matmul_mx(
-                        out=acc2[f][:, nt, :],
-                        lhsT=w2w[:, f * 2 * N + nt * 2 * P : f * 2 * N + (nt + 1) * 2 * P].bitcast(FP4X4),
-                        lhsT_scale=w2s[:, f * N + nt * P : f * N + (nt + 1) * P],
-                        rhs=cq[:, i * C2 : (i + 1) * C2].bitcast(FP8X4),
-                        rhs_scale=cs[:, i * C2 : (i + 1) * C2],
+                        out=acc2[f][:, r, :],
+                        lhsT=w2w[:, 2 * col : 2 * (col + P)].bitcast(FP4X4),
+                        lhsT_scale=w2s[:, col : col + P],
+                        rhs=codes[:, nth * C2 : (nth + 1) * C2].bitcast(FP8X4),
+                        rhs_scale=scales[:, nth * C2 : (nth + 1) * C2],
                         start=True,
                         stop=True,
                     )
 
-        ow = [keep.tile([P, T], F32, name="ow%d" % nt) for nt in range(4)]
+        result = [keep.tile([P, T], F32, name="result%d" % r) for r in range(PACK)]
 
-        def back2(c, pair):
-            lo, hi = CHUNKS[c][0] * C2, CHUNKS[c][1] * C2
+        def scatter2(ch, pair):
+            lo, hi = CHUNKS[ch][0] * C2, CHUNKS[ch][1] * C2
             y = ring4.tile([P, 2, hi - lo], F32, name="y")
-            for i, f in enumerate(range(*CHUNKS[c])):
-                nc.scalar.copy(y[:, :, i * C2 : (i + 1) * C2], acc2[f][:, 2 * pair : 2 * pair + 2, :])
-            for nt in range(2 * pair, 2 * pair + 2):
-                nc.vector.tensor_tensor(ow[nt][:].indirect(list2[:, cols16(lo, hi)]), y[:, nt % 2, :], g2[:, lo:hi], MULT)
-                if c == len(CHUNKS) - 1:
-                    nc.sync.dma_start(out=out[nt * P : (nt + 1) * P, :], in_=ow[nt][:])
+            for nth, f in enumerate(range(*CHUNKS[ch])):
+                nc.scalar.copy(y[:, :, nth * C2 : (nth + 1) * C2], acc2[f][:, 2 * pair : 2 * pair + 2, :])
+            for r in range(2 * pair, 2 * pair + 2):
+                nc.vector.tensor_tensor(result[r][:].indirect(list2[:, entries(lo, hi)]), y[:, r % 2, :], g2[:, lo:hi], MULT)
+                if ch == len(CHUNKS) - 1:
+                    nc.sync.dma_start(out=out[r * P : (r + 1) * P, :], in_=result[r][:])
 
-        gather_words(0, 0)
-        gather_words(0, 1)
-        gather_words(1, 0)
-        gather_words(1, 1)
+        for a in range(LAST_PASS):
+            gather_words(a, 0)
+            gather_words(a, 1)
         gather_scales(0)
         gather_scales(1)
-        pass1(0, 0)
-        pass1(0, 1)
-        gather_words(2, 0)
-        pass1(0, 2)
-        gather_words(2, 1)
+        layer1_pass(0, 0)
+        layer1_pass(0, 1)
+        gather_words(LAST_PASS, 0)
+        layer1_pass(0, LAST_PASS)
+        gather_words(LAST_PASS, 1)
         for e in range(E1 - 1):
-            back1(e, 0)
-            back1(e, 1)
+            scatter1(e, 0)
+            scatter1(e, 1)
             if e == 0:
-                pass1(1, 0)
-            pass1(e + 1, 1)
-            back1(e, 2)
-            pass1(e + 1, 2)
-            back1(e, 3)
+                layer1_pass(1, 0)
+            layer1_pass(e + 1, 1)
+            scatter1(e, 2)
+            layer1_pass(e + 1, LAST_PASS)
+            scatter1(e, 3)
             if e + 2 < E1:
-                pass1(e + 2, 0)
-        for t in range(4):
-            back1(E1 - 1, t)
-        for t in range(4):
-            nc.scalar.copy(cb[t][:], cw[t][:])
+                layer1_pass(e + 2, 0)
+        for t in range(PACK):
+            scatter1(E1 - 1, t)
+
+        for t in range(PACK):
+            nc.scalar.copy(c16[t][:], c32[t][:])
             gather2(0, t)
         layer2(0)
-        for c in range(len(CHUNKS)):
-            back2(c, 0)
-            if c + 1 < len(CHUNKS):
-                for t in range(4):
-                    gather2(c + 1, t)
-                layer2(c + 1)
-            back2(c, 1)
+        for ch in range(len(CHUNKS)):
+            scatter2(ch, 0)
+            if ch + 1 < len(CHUNKS):
+                for t in range(PACK):
+                    gather2(ch + 1, t)
+                layer2(ch + 1)
+            scatter2(ch, 1)

from contextlib import ExitStack

import concourse.mybir as mybir

K, T, H, N = 1536, 1024, 512, 512
E1, C1, E2, C2 = 4, 256, 8, 128
FLOPS = 2 * T * (K * H + H * N)

F32 = mybir.dt.float32
BF16 = mybir.dt.bfloat16
I32 = mybir.dt.int32
U32 = mybir.dt.uint32
U16 = mybir.dt.uint16
U8 = mybir.dt.uint8
FP8X4 = mybir.dt.float8_e4m3fn_x4
FP4X4 = mybir.dt.float4_e2m1fn_x4
COPY = mybir.ActivationFunctionType.Copy
MULT = mybir.AluOpType.mult

P = 128
PACK = 4
K_PASS = P * PACK
PASSES = K // K_PASS
LAST_PASS = PASSES - 1
HALF = H // 2
QUADRANTS = 4
ALIGN = 64
SLAB = 4096

PARTS = ((0, C1), (C1, T))
CHUNKS = ((0, 1), (1, 2), (2, 4), (4, 6), (6, 8))
EARLY_CHUNKS = 2
HALVED = ((0, LAST_PASS), (1, 0))
ON_VECTOR = ((0, LAST_PASS, 1), (2, 1, 1))


def entries(lo, hi):
    return slice(lo // 16, hi // 16)


def tile_moe_ser_none_kernel(
    tc, x_words, x_scales, w1, w2_words, w2_scales, gate1, gate2, offs, offs2, out
):
    nc = tc.nc
    with ExitStack() as ctx:
        keep = ctx.enter_context(tc.tile_pool(name="keep", bufs=1))
        loads = ctx.enter_context(tc.tile_pool(name="loads", bufs=10))
        ring3 = ctx.enter_context(tc.tile_pool(name="ring3", bufs=3))
        ring4 = ctx.enter_context(tc.tile_pool(name="ring4", bufs=4))
        shared = ctx.enter_context(tc.tile_pool(name="shared", bufs=1))
        psum = ctx.enter_context(tc.psum_pool(name="psum", bufs=2))

        list1 = keep.tile([P, T // 16], U16, name="list1")
        list2 = keep.tile([P, T // 16], U16, name="list2")
        xw = [
            keep.tile([P, T], I32, name="xw0", align_bytes=ALIGN),
            shared.tile([P, T], I32, name="xw1", align_bytes=ALIGN, offset=0),
            keep.tile([P, T], I32, name="xw2", align_bytes=ALIGN),
        ]
        xs = keep.tile([P, T], U8, name="xs", align_bytes=ALIGN)
        w2w = keep.tile([P, E2 * 2 * N], U8, name="w2w", align_bytes=ALIGN)
        w2s = keep.tile([P, E2 * N], U8, name="w2s", align_bytes=ALIGN)
        g1 = [keep.tile([P, C1], F32, name="g1_%d" % e) for e in range(E1)]
        g2 = keep.tile([P, T], F32, name="g2")

        nc.vector.memset(xs[:].bitcast(I32), 0)
        nc.vector.memset(w2s[:].bitcast(I32), 0)

        raw = {}

        def load_w1(e, a, half=None):
            rows = w1[e, K_PASS * a : K_PASS * (a + 1), :].rearrange("(p j) i -> p j i", j=PACK)
            if half != 1:
                raw[(e, a)] = loads.tile([P, PACK, H], F32, name="raw")
            cols = slice(0, H) if half is None else slice(half * HALF, (half + 1) * HALF)
            nc.sync.dma_start(out=raw[(e, a)][:, :, cols], in_=rows[:, :, cols])

        def load_xw(a):
            nc.sync.dma_start(out=xw[a][:], in_=x_words[a].rearrange("p t d -> p (t d)").bitcast(I32))

        def load_xs(q):
            for lo, hi in ((0, 2), (2, PASSES)):
                nc.sync.dma_start(
                    out=xs[32 * q + 4 * lo : 32 * q + 4 * hi, :].bitcast(I32),
                    in_=x_scales[lo:hi, 4 * q : 4 * q + 4, :].bitcast(I32),
                )

        load_xw(0)
        nc.sync.dma_start(list1[:], offs)
        load_xs(0)
        load_xw(1)
        load_xs(1)
        load_w1(0, 0)
        load_xs(2)
        load_xs(3)
        load_w1(0, 1)
        load_w1(0, LAST_PASS, 0)
        load_w1(0, LAST_PASS, 1)
        load_w1(1, 0, 0)
        load_xw(LAST_PASS)
        load_w1(1, 0, 1)
        for e in range(E1):
            nc.sync.dma_start(out=g1[e][:], in_=gate1[:, e * C1 : (e + 1) * C1])
            if e + 1 < E1:
                for a in range(1, PASSES):
                    load_w1(e + 1, a)
            if e + 2 < E1:
                load_w1(e + 2, 0)
        nc.sync.dma_start(list2[:], offs2)
        for q in range(QUADRANTS):
            nc.sync.dma_start(
                out=w2s[32 * q : 32 * q + 4, :].bitcast(I32).rearrange("r (f n) -> r f n", f=E2),
                in_=w2_scales[:, 0, 4 * q : 4 * q + 4, :].bitcast(I32).rearrange("f r n -> r f n"),
            )
        nc.sync.dma_start(
            out=w2w[:].bitcast(I32).rearrange("p (f n) -> p f n", f=E2),
            in_=w2_words[:, 0, :, :].bitcast(I32).rearrange("f p n -> p f n"),
        )
        nc.sync.dma_start(out=g2[:], in_=gate2)

        gw = {}
        gs = {}

        def gather_words(a, part):
            lo, hi = PARTS[part]
            name = "gw%d_%d" % (a, part)
            if a == LAST_PASS:
                gw[(a, part)] = shared.tile([P, hi - lo], U32, name=name, align_bytes=ALIGN, offset=SLAB * (1 + part))
            else:
                gw[(a, part)] = keep.tile([P, hi - lo], U32, name=name, align_bytes=ALIGN)
            nc.vector.tensor_copy(gw[(a, part)][:], xw[a][:].bitcast(U32).indirect(list1[:, entries(lo, hi)]))

        def gather_scales(part):
            lo, hi = PARTS[part]
            gs[part] = shared.tile([P, hi - lo], U8, name="gs%d" % part, align_bytes=ALIGN, offset=lo)
            nc.vector.tensor_copy(gs[part][:], xs[:].indirect(list1[:, entries(lo, hi)]))

        c32 = [keep.tile([P, T], F32, name="c32_%d" % t) for t in range(PACK)]
        c16 = [keep.tile([P, T], BF16, name="c16_%d" % t) for t in range(PACK)]
        acc1 = {}

        def layer1_pass(e, a):
            if e == 0 and a > 0:
                stage = shared.tile([P, PACK, P, PACK], BF16, name="stage0_%d" % a, align_bytes=ALIGN, offset=SLAB * a)
            else:
                stage = ring4.tile([P, PACK, P, PACK], BF16, name="stage", align_bytes=ALIGN)
            dst = stage[:].rearrange("p t m j -> p m j t")
            src = raw[(e, a)][:].rearrange("p j (m t) -> p m j t", t=PACK)
            for half in range(2):
                copy = nc.vector.tensor_copy if (e, a, half) in ON_VECTOR else nc.scalar.copy
                if (e, a) in HALVED:
                    ms = slice(half * P // 2, (half + 1) * P // 2)
                    copy(dst[:, ms, :, :], src[:, ms, :, :])
                else:
                    ts = slice(2 * half, 2 * half + 2)
                    copy(dst[:, :, :, ts], src[:, :, :, ts])
            codes = ring4.tile([P, H], U32, name="w1_codes", align_bytes=ALIGN)
            scales = ring4.tile([P, H], U8, name="w1_scales", align_bytes=ALIGN)
            nc.vector.quantize_mx(
                out=codes[:].bitcast(FP8X4), scales=scales[:], in_=stage[:].rearrange("p t m j -> p (t m j)")
            )
            part = min(e, 1)
            at = e * C1 - PARTS[part][0]
            for t in range(PACK):
                if a == 0:
                    acc1[(e, t)] = psum.tile([P, C1], F32, name="bank%d" % t)
                nc.tensor.matmul_mx(
                    out=acc1[(e, t)][:],
                    lhsT=codes[:, t * P : (t + 1) * P].bitcast(FP8X4),
                    lhsT_scale=scales[:, t * P : (t + 1) * P],
                    rhs=gw[(a, part)][:, at : at + C1].bitcast(FP8X4),
                    rhs_scale=gs[part][4 * a : P, at : at + C1],
                    start=(a == 0),
                    stop=(a == LAST_PASS),
                )

        def scatter1(e, t):
            if t == PACK - 1 and e + 1 < E1:
                h = raw[(e + 1, LAST_PASS)][:, PACK - 1, H - C1 : H]
            else:
                h = ring4.tile([P, C1], F32, name="h")[:]
            nc.scalar.copy(h, acc1[(e, t)][:])
            nc.vector.tensor_tensor(c32[t][:].indirect(list1[:, entries(e * C1, (e + 1) * C1)]), h, g1[e][:], MULT)

        slots16 = {}

        def gather2(ch, t):
            lo, hi = CHUNKS[ch][0] * C2, CHUNKS[ch][1] * C2
            if t == 0:
                slots16[ch] = ring3.tile([P, hi - lo, PACK], BF16, name="slots16", align_bytes=ALIGN)
            if ch < EARLY_CHUNKS and t >= 2:
                nc.vector.tensor_copy(slots16[ch][:, :, t], c32[t][:].indirect(list2[:, entries(lo, hi)]))
            else:
                nc.scalar.activation(slots16[ch][:, :, t], c16[t][:].indirect(list2[:, entries(lo, hi)]), COPY)

        acc2 = {}

        def layer2(ch):
            width = (CHUNKS[ch][1] - CHUNKS[ch][0]) * C2
            codes = ring3.tile([P, width], U32, name="c_codes", align_bytes=ALIGN)
            scales = ring3.tile([P, width], U8, name="c_scales", align_bytes=ALIGN)
            nc.vector.quantize_mx(
                out=codes[:].bitcast(FP8X4), scales=scales[:], in_=slots16[ch][:].rearrange("p m t -> p (m t)")
            )
            for nth, f in enumerate(range(*CHUNKS[ch])):
                acc2[f] = psum.tile([P, PACK, C2], F32, name="bank%d" % (f % PACK))
                for r in range(PACK):
                    col = f * N + r * P
                    nc.tensor.matmul_mx(
                        out=acc2[f][:, r, :],
                        lhsT=w2w[:, 2 * col : 2 * (col + P)].bitcast(FP4X4),
                        lhsT_scale=w2s[:, col : col + P],
                        rhs=codes[:, nth * C2 : (nth + 1) * C2].bitcast(FP8X4),
                        rhs_scale=scales[:, nth * C2 : (nth + 1) * C2],
                        start=True,
                        stop=True,
                    )

        result = [keep.tile([P, T], F32, name="result%d" % r) for r in range(PACK)]

        def scatter2(ch, pair):
            lo, hi = CHUNKS[ch][0] * C2, CHUNKS[ch][1] * C2
            y = ring4.tile([P, 2, hi - lo], F32, name="y")
            for nth, f in enumerate(range(*CHUNKS[ch])):
                nc.scalar.copy(y[:, :, nth * C2 : (nth + 1) * C2], acc2[f][:, 2 * pair : 2 * pair + 2, :])
            for r in range(2 * pair, 2 * pair + 2):
                nc.vector.tensor_tensor(result[r][:].indirect(list2[:, entries(lo, hi)]), y[:, r % 2, :], g2[:, lo:hi], MULT)
                if ch == len(CHUNKS) - 1:
                    nc.sync.dma_start(out=out[r * P : (r + 1) * P, :], in_=result[r][:])

        for a in range(LAST_PASS):
            gather_words(a, 0)
            gather_words(a, 1)
        gather_scales(0)
        gather_scales(1)
        layer1_pass(0, 0)
        layer1_pass(0, 1)
        gather_words(LAST_PASS, 0)
        layer1_pass(0, LAST_PASS)
        gather_words(LAST_PASS, 1)
        for e in range(E1 - 1):
            scatter1(e, 0)
            scatter1(e, 1)
            if e == 0:
                layer1_pass(1, 0)
            layer1_pass(e + 1, 1)
            scatter1(e, 2)
            layer1_pass(e + 1, LAST_PASS)
            scatter1(e, 3)
            if e + 2 < E1:
                layer1_pass(e + 2, 0)
        for t in range(PACK):
            scatter1(E1 - 1, t)

        for t in range(PACK):
            nc.scalar.copy(c16[t][:], c32[t][:])
            gather2(0, t)
        layer2(0)
        for ch in range(len(CHUNKS)):
            scatter2(ch, 0)
            if ch + 1 < len(CHUNKS):
                for t in range(PACK):
                    gather2(ch + 1, t)
                layer2(ch + 1)
            scatter2(ch, 1)
